import numpy as np
import ml_dtypes


def mxq(x, axis, fmt="e4m3"):
    dtype, down = {"e4m3": (ml_dtypes.float8_e4m3fn, 7), "e5m2": (ml_dtypes.float8_e5m2, 14)}[fmt]
    v = np.moveaxis(np.asarray(x, np.float32).astype(ml_dtypes.bfloat16).astype(np.float64), axis, -1)
    blocks = v.reshape(v.shape[:-1] + (-1, 32))
    amax = np.abs(blocks).max(-1, keepdims=True)
    byte = np.maximum(np.where(amax > 0, np.frexp(amax)[1] - 1 + 127, 0) - down, 1)
    scale = np.exp2(byte - 127.0)
    codes = (blocks / scale).astype(np.float32).astype(dtype).astype(np.float64)
    return np.moveaxis((codes * scale).reshape(v.shape), -1, axis)


WIDE = False


def mx_kscale(k):
    if not WIDE:
        return np.ones(k)
    levels = np.array([10, -10, 5, -5, 0])
    if k % 512:
        return np.exp2(np.random.permutation(np.resize(levels, k // 32))).repeat(32)
    a = np.empty((k // 512, 16))
    for p in range(k // 512):
        a[p, :8] = np.random.permutation(np.resize(levels, 8))
        for g in range(8):
            far = levels[np.abs(levels - a[p, g]) >= 10]
            a[p, g + 8] = far[np.random.randint(len(far))]
    return np.exp2(a.ravel()).repeat(32)


def f64(x):
    return np.asarray(x).astype(np.float64)


def striped(idx):
    return np.tile(idx.reshape(-1, 16).T, (8, 1)).astype(np.uint16)


def unstriped(offs):
    return offs[:16].T.reshape(-1).astype(np.int64)


E2M1 = np.array([0.0, 0.5, 1.0, 1.5, 2.0, 3.0, 4.0, 6.0, -0.0, -0.5, -1.0, -1.5, -2.0, -3.0, -4.0, -6.0])


def pack_weight(w, fmt):
    k, n = w.shape
    w = f64(np.asarray(w, np.float32).astype(ml_dtypes.bfloat16)).reshape(k // 32, 32, n)
    amax = np.abs(w).max(1)
    if fmt == "e4m3":
        byte = np.frexp(amax)[1] - 1 + 127 - 7
    else:
        mant, ex = np.frexp(amax / 6.0)
        byte = np.where(mant > 0.5, ex, ex - 1) + 127
    byte = np.clip(np.where(amax > 0, byte, 1), 1, 254)
    scaled = (w * np.exp2(127.0 - byte)[:, None, :]).reshape(k, n).astype(np.float32)
    by_word = np.ascontiguousarray(scaled.reshape(k // 512, 128, 4, n).transpose(0, 1, 3, 2))
    if fmt == "e4m3":
        words = by_word.astype(ml_dtypes.float8_e4m3fn).view(np.uint8)
    else:
        c = by_word.astype(ml_dtypes.float4_e2m1fn).view(np.uint8) & 0xF
        words = (c[..., 0::2] | (c[..., 1::2] << 4)).reshape(k // 512, 128, 2 * n)
    return np.ascontiguousarray(words), np.ascontiguousarray(byte.astype(np.uint8).reshape(k // 512, 16, n))


def unpack_weight(words, scales, fmt):
    g, _, n = scales.shape
    words = np.ascontiguousarray(words).reshape(g, 128, n, -1)
    if fmt == "e4m3":
        vals = words.view(ml_dtypes.float8_e4m3fn).astype(np.float64)
    else:
        nib = np.empty((g, 128, n, 4), np.uint8)
        nib[..., 0::2] = words & 0xF
        nib[..., 1::2] = words >> 4
        vals = E2M1[nib]
    vals = vals * np.repeat(np.exp2(scales.astype(np.float64) - 127.0), 8, axis=1)[..., None]
    return vals.transpose(0, 1, 3, 2).reshape(g * 512, n)


def gelu(v):
    return 0.5 * v * (1.0 + np.tanh(np.sqrt(2.0 / np.pi) * (v + 0.044715 * v**3)))


def bf(x):
    return np.asarray(x, np.float32).astype(ml_dtypes.bfloat16)


def planes(Y):
    n, m = Y.shape
    b = f64(bf(Y)).reshape(n // 32, 32, m)
    amax = np.abs(b).max(1)
    byte = np.clip(np.where(amax > 0, np.frexp(amax)[1] - 1 + 127 - 7, 1), 1, 254)
    codes = (b * np.exp2(127.0 - byte)[:, None, :]).reshape(n, m).astype(np.float32).astype(ml_dtypes.float8_e4m3fn).view(np.uint8)
    words = codes.reshape(n // 512, 128, 4, m).transpose(0, 1, 3, 2)
    return np.ascontiguousarray(words), np.ascontiguousarray(byte.astype(np.uint8).reshape(n // 512, 16, m))


K, H, N, T, S, P = 1536, 512, 1024, 2048, 1024, 512


def setup_inputs():
    n = np.random.standard_normal
    s = mx_kscale(K)[:, None]
    u = mx_kscale(H)[:, None]
    tab_words, tab_scales = pack_weight(n((K, T)) * s, "e4m3")
    w2_words, w2_scales = pack_weight(0.9 * n((K, H)) / np.sqrt(K) / s, "e2m1")
    w1 = 0.9 * n((K, H)) / np.sqrt(K) / s
    w6 = 2.0 * n((H, N)) / np.sqrt(H) * np.exp(0.8 * n(N))[None, :] / u
    return {
        "tab_words": tab_words, "tab_scales": tab_scales,
        "offs": striped(np.random.permutation(T)[:S]),
        "pos1": striped(np.random.permutation(S)[:P]),
        "pos2": striped(np.random.permutation(S)[:P]),
        "w1": w1.astype(np.float32),
        "w2_words": w2_words, "w2_scales": w2_scales,
        "w6": w6.astype(np.float32),
        "sharp": np.random.uniform(1, 3, H).astype(np.float32),
        "share": np.random.uniform(0.1, 0.5, H).astype(np.float32),
        "base": np.random.uniform(0.1, 0.9, H).astype(np.float32),
        "tilt": (0.12 * n(H)).astype(np.float32),
        "turn": (5.0 * n((H, P)) * u).astype(np.float32),
    }


def reference(tab_words, tab_scales, offs, pos1, pos2, w1, w2_words, w2_scales, w6,
              sharp, share, base, tilt, turn):
    v = unpack_weight(tab_words, tab_scales, "e4m3")[:, unstriped(offs)]
    h = mxq(f64(w1), 0, "e4m3").T @ v
    g = unpack_weight(w2_words, w2_scales, "e2m1").T @ v
    top = h.max(axis=1)
    a = 1.0 / (1.0 + np.exp(-f64(sharp)[:, None] * (h[:, unstriped(pos1)] - f64(share)[:, None] * top[:, None])))
    peak = g.max(axis=1)
    c = np.exp(g[:, unstriped(pos2)] - peak[:, None])
    z = (a - f64(base)[:, None]) * (c - f64(tilt)[:, None]) * f64(turn)
    y = mxq(f64(w6), 0, "e4m3").T @ mxq(z, 0, "e4m3")
    words, scales = planes(y)
    return y, words, scales

@@ -1,0 +1,299 @@
+from contextlib import ExitStack
+
+import concourse.mybir as mybir
+
+K, H, N, T, S, PICK = 1536, 512, 1024, 2048, 1024, 512
+FLOPS = 2 * (2 * K * H * S + H * N * PICK)
+
+F32 = mybir.dt.float32
+BF16 = mybir.dt.bfloat16
+I32 = mybir.dt.int32
+U32 = mybir.dt.uint32
+U16 = mybir.dt.uint16
+U8 = mybir.dt.uint8
+FP8X4 = mybir.dt.float8_e4m3fn_x4
+FP4X4 = mybir.dt.float4_e2m1fn_x4
+ALU = mybir.AluOpType
+ACT = mybir.ActivationFunctionType
+
+P = 128
+PACK = 4
+PASSES = K // (P * PACK)
+BANK = 512
+HALF = PICK // 2
+GROUPS = N // (P * PACK)
+LIVE = 32 - 4 * PASSES
+
+
+def tile_list_discard_danger_kernel(
+    tc, tab_words, tab_scales, offs, pos1, pos2, w1, w2_words, w2_scales, w6,
+    sharp, share, base, tilt, turn, out_0, out_1, out_2,
+):
+    nc = tc.nc
+    with ExitStack() as ctx:
+        sb = ctx.enter_context(tc.tile_pool(name="sb", bufs=1))
+        ps = ctx.enter_context(tc.psum_pool(name="ps", bufs=1))
+
+        def tile(name, shape, dtype, tag=None):
+            return sb.tile(shape, dtype, name=name, tag=tag or name, align_bytes=64)
+
+        def bank(name, b):
+            return ps.tile([P, BANK], F32, name=name, tag="bank%d" % b)
+
+        offs_sb = sb.tile([P, S // 16], U16, name="offs_sb")
+        pos1_sb = sb.tile([P, PICK // 16], U16, name="pos1_sb")
+        pos2_sb = sb.tile([P, PICK // 16], U16, name="pos2_sb")
+
+        def streamed(name, shape, dtype):
+            return sb.tile(shape, dtype, name=name, tag="stream", bufs=3, align_bytes=64)
+
+        tab_s = tile("tab_s", [P, T], U8)
+        w2_s_raw = tile("w2_s_raw", [P, PASSES, H], U8)
+        v_s_packed = tile("v_s_packed", [P, S], U8)
+        v_s = [tile("v_s%d" % a, [P, S], U8) for a in range(PASSES)]
+        nc.vector.memset(w2_s_raw[:].bitcast(I32), 0)
+        for q in range(4):
+            nc.vector.memset(tab_s[32 * q : 32 * q + LIVE, :].bitcast(I32), 0)
+        for a in range(PASSES):
+            nc.vector.memset(v_s[a][:].bitcast(I32), 0)
+
+        nc.sync.dma_start(offs_sb[:], offs)
+        nc.sync.dma_start(pos2_sb[:], pos2)
+        nc.sync.dma_start(pos1_sb[:], pos1)
+        for q in range(4):
+            nc.scalar.dma_start(
+                out=tab_s[32 * q + LIVE : 32 * (q + 1), :].bitcast(I32),
+                in_=tab_scales[:, 4 * q : 4 * q + 4, :].bitcast(I32),
+            )
+
+        tab_w = [streamed("tab_w%d" % a, [P, T], I32) for a in range(PASSES)]
+        w2_raw = tile("w2_raw", [P, PASSES, 2 * H], U8)
+
+        def load_tab(a):
+            nc.sync.dma_start(out=tab_w[a][:], in_=tab_words[a].rearrange("p t i -> p (t i)").bitcast(I32))
+
+        load_tab(0)
+        nc.sync.dma_start(out=w2_raw[:].bitcast(I32), in_=w2_words.rearrange("a p n -> p a n").bitcast(I32))
+        for q in range(4):
+            nc.sync.dma_start(
+                out=w2_s_raw[32 * q : 32 * q + 4, :, :].bitcast(I32),
+                in_=w2_scales[:, 4 * q : 4 * q + 4, :].rearrange("a r n -> r a n").bitcast(I32),
+            )
+        load_tab(1)
+        load_tab(2)
+
+        nc.vector.tensor_copy(out=v_s_packed[:], in_=tab_s[:].indirect(offs_sb[:]))
+        for a in range(PASSES):
+            first = LIVE + 4 * a
+            nc.scalar.dma_start(
+                out=v_s[a][0 : P - first, :].bitcast(I32), in_=v_s_packed[first:P, :].bitcast(I32)
+            )
+        w2_s = tile("w2_s", [P, PASSES, H], U8)
+        nc.vector.tensor_copy(
+            out=w2_s[:].rearrange("p a (t m) -> p a t m", t=PACK),
+            in_=w2_s_raw[:].rearrange("p a (m t) -> p a t m", t=PACK),
+        )
+        w2_c = tile("w2_c", [P, PASSES, 2 * H], U8)
+        nc.scalar.copy(
+            out=w2_c[:].bitcast(U16).rearrange("p a (t m) -> p a t m", t=PACK),
+            in_=w2_raw[:].bitcast(U16).rearrange("p a (m t) -> p a t m", t=PACK),
+        )
+
+        def load_rows(name, rows_ap):
+            raw = streamed(name, [P, PACK, H], F32)
+            nc.sync.dma_start(out=raw[:], in_=rows_ap)
+            return raw
+
+        w1_raw = [
+            load_rows("w1_raw%d" % a, w1[a * P * PACK : (a + 1) * P * PACK, :].rearrange("(p i) r -> p i r", i=PACK))
+            for a in range(PASSES)
+        ]
+        row_values = tile("row_values", [P, 4, 8], F32, "v_s_packed")
+        rows = {}
+        for n, (name, vec) in enumerate((("tilt", tilt), ("sharp", sharp), ("share", share), ("base", base))):
+            rows[name] = row_values[:, n, 0:PACK]
+            nc.sync.dma_start(out=rows[name], in_=vec.rearrange("(p t) -> p t", t=PACK))
+        turn_sb = load_rows("turn_sb", turn.rearrange("(p t) m -> p t m", t=PACK))
+        w6_raw = [
+            load_rows("w6_raw%d" % g, w6.rearrange("(p i) n -> p i n", i=PACK)[:, :, g * H : (g + 1) * H])
+            for g in range(GROUPS)
+        ]
+
+        v_w = [[tile("v_w%d_%d" % (a, j), [P, BANK], U32) for j in range(2)] for a in range(PASSES)]
+        g_bank = [[bank("g_ps%d_%d" % (t, j), 2 * t + j) for j in range(2)] for t in range(PACK)]
+        for a in range(PASSES):
+            for j in range(2):
+                nc.vector.tensor_copy(
+                    out=v_w[a][j][:],
+                    in_=tab_w[a][:].bitcast(U32).indirect(offs_sb[:, j * BANK // 16 : (j + 1) * BANK // 16]),
+                )
+
+        def g_pass(a, t, j):
+            nc.tensor.matmul_mx(
+                out=g_bank[t][j][:],
+                lhsT=w2_c[:, a, 2 * P * t : 2 * P * (t + 1)].bitcast(FP4X4),
+                lhsT_scale=w2_s[:, a, P * t : P * (t + 1)],
+                rhs=v_w[a][j][:].bitcast(FP8X4),
+                rhs_scale=v_s[a][:, j * BANK : (j + 1) * BANK],
+                start=(a == 0),
+                stop=(a == PASSES - 1),
+            )
+
+        for a in range(PASSES - 1):
+            for j in range(2):
+                for t in range(PACK):
+                    g_pass(a, t, j)
+        for t in range(PACK):
+            for j in range(2):
+                g_pass(PASSES - 1, t, j)
+
+        def round_weight(engine_copy, name, raw):
+            dealt = tile(name + "_bf", [P, PACK * H], BF16)
+            engine_copy(
+                out=dealt[:].rearrange("p (t m i) -> p m t i", t=PACK, i=PACK),
+                in_=raw[:].rearrange("p i (m t) -> p m t i", t=PACK),
+            )
+            return dealt
+
+        def quantise(name, values, width):
+            codes = tile(name + "_c", [P, width], U32)
+            scales = tile(name + "_s", [P, width], U8)
+            nc.vector.quantize_mx(out=codes[:].bitcast(FP8X4), scales=scales[:], in_=values[:])
+            return codes, scales
+
+        def empty(name, banks, tag=None):
+            whole = tile(name, [P, S], F32, tag)
+            top = tile(name + "_top", [P, 2], F32)
+            for j in range(2):
+                nc.vector.tensor_scalar(
+                    out=whole[:, j * BANK : (j + 1) * BANK], in0=banks[j][:], scalar1=1.0, scalar2=None,
+                    op0=ALU.mult, op1=ALU.max, accum_out=top[:, j : j + 1],
+                )
+            return whole, top
+
+        def scalar_round(out, in_):
+            nc.scalar.activation(out=out, in_=in_, func=ACT.Copy)
+
+        w1_bf = [round_weight(scalar_round, "w1_%d" % a, w1_raw[a]) for a in range(2)]
+
+        exp_bias = tile("exp_bias", [P, PACK], F32)
+        c_sb = []
+        for t in range(PACK):
+            g_sb, top = empty("g%d" % t, g_bank[t])
+            nc.vector.tensor_scalar(
+                out=exp_bias[:, t : t + 1], in0=top[:, 0:1], scalar1=top[:, 1:2], scalar2=-1.0,
+                op0=ALU.max, op1=ALU.mult,
+            )
+            c_t = tile("c%d" % t, [P, PICK], F32)
+            nc.scalar.activation(
+                out=c_t[:], in_=g_sb[:].indirect(pos2_sb[:]), func=ACT.Exp, bias=exp_bias[:, t : t + 1]
+            )
+            c_sb.append(c_t)
+
+        w1_q = [quantise("w1_%d" % a, w1_bf[a], H) for a in range(2)]
+        w1_bf.append(round_weight(nc.vector.tensor_copy, "w1_2", w1_raw[2]))
+        gain = tile("gain", [P, PACK], F32)
+        nc.vector.scalar_tensor_tensor(
+            out=gain[:], in0=rows["sharp"], scalar=-1.0, in1=rows["share"], op0=ALU.mult, op1=ALU.mult
+        )
+        w1_q.append(quantise("w1_2", w1_bf[2], H))
+
+        h_bank = [[bank("h_ps%d_%d" % (t, j), 2 * t + j) for j in range(2)] for t in range(PACK)]
+        for a in range(PASSES):
+            for t in range(PACK):
+                for j in range(2):
+                    nc.tensor.matmul_mx(
+                        out=h_bank[t][j][:],
+                        lhsT=w1_q[a][0][:, P * t : P * (t + 1)].bitcast(FP8X4),
+                        lhsT_scale=w1_q[a][1][:, P * t : P * (t + 1)],
+                        rhs=v_w[a][j][:].bitcast(FP8X4),
+                        rhs_scale=v_s[a][:, j * BANK : (j + 1) * BANK],
+                        start=(a == 0),
+                        stop=(a == PASSES - 1),
+                    )
+
+
+        w6_bf = [round_weight(scalar_round, "w6_0", w6_raw[0])]
+        sig_bias = tile("sig_bias", [P, PACK], F32)
+        a_sb = []
+        for t in range(PACK):
+            h_sb, top = empty("h%d" % t, h_bank[t])
+            nc.vector.tensor_scalar(
+                out=sig_bias[:, t : t + 1], in0=top[:, 0:1], scalar1=top[:, 1:2], scalar2=gain[:, t : t + 1],
+                op0=ALU.max, op1=ALU.mult,
+            )
+            halves = []
+            for c in range(2):
+                a_t = tile("a%d_%d" % (t, c), [P, HALF], F32)
+                nc.scalar.activation(
+                    out=a_t[:], in_=h_sb[:].indirect(pos1_sb[:, c * HALF // 16 : (c + 1) * HALF // 16]),
+                    func=ACT.Sigmoid, bias=sig_bias[:, t : t + 1], scale=rows["sharp"][:, t : t + 1],
+                )
+                halves.append(a_t)
+            a_sb.append(halves)
+
+        w6_bf.append(round_weight(nc.vector.tensor_copy, "w6_1", w6_raw[1]))
+        weighted = []
+        for t in range(PACK):
+            w_t = tile("weighted%d" % t, [P, PICK], F32)
+            nc.vector.scalar_tensor_tensor(
+                out=w_t[:], in0=c_sb[t][:], scalar=rows["tilt"][:, t : t + 1], in1=turn_sb[:, t, :],
+                op0=ALU.subtract, op1=ALU.mult,
+            )
+            weighted.append(w_t)
+        w6_q = [quantise("w6_%d" % g, w6_bf[g], H) for g in range(GROUPS)]
+
+        z_q = []
+        for c in range(2):
+            z_rows = tile("z_rows%d" % c, [P, PACK, HALF], BF16)
+            for t in range(PACK):
+                nc.vector.scalar_tensor_tensor(
+                    out=z_rows[:, t, :], in0=a_sb[t][c][:], scalar=rows["base"][:, t : t + 1],
+                    in1=weighted[t][:, c * HALF : (c + 1) * HALF], op0=ALU.subtract, op1=ALU.mult,
+                )
+            z_bf = tile("z_bf%d" % c, [P, PACK * HALF], BF16)
+            nc.vector.tensor_copy(
+                out=z_bf[:].rearrange("p (c i t) -> p c t i", i=4, t=PACK),
+                in_=z_rows[:].rearrange("p t (c i) -> p c t i", i=4),
+            )
+            z_q.append(quantise("z%d" % c, z_bf, HALF))
+
+        y_s = tile("y_s", [P, GROUPS, PICK], U8)
+        y_rows = out_0.rearrange("(g p t) m -> g p t m", p=P, t=PACK)
+        for c in range(2):
+            cols = slice(c * HALF, (c + 1) * HALF)
+            for g in range(GROUPS):
+                y_sb = tile("y%d_%d" % (g, c), [P, PACK, HALF], F32)
+                for u in range(2):
+                    y_ps = bank("y_ps%d_%d_%d" % (c, g, u), 4 * c + 2 * g + u)
+                    for e in range(2):
+                        t = 2 * u + e
+                        nc.tensor.matmul_mx(
+                            out=y_ps[:, e * HALF : (e + 1) * HALF],
+                            lhsT=w6_q[g][0][:, P * t : P * (t + 1)].bitcast(FP8X4),
+                            lhsT_scale=w6_q[g][1][:, P * t : P * (t + 1)],
+                            rhs=z_q[c][0][:].bitcast(FP8X4),
+                            rhs_scale=z_q[c][1][:],
+                            start=True,
+                            stop=True,
+                        )
+                    nc.scalar.copy(
+                        out=y_sb[:, 2 * u : 2 * u + 2, :], in_=y_ps[:].rearrange("p (e m) -> p e m", e=2)
+                    )
+                nc.sync.dma_start(out=y_rows[g][:, :, cols], in_=y_sb[:])
+                y_bf = tile("y_bf%d_%d" % (g, c), [P, PACK * HALF], BF16)
+                nc.vector.tensor_copy(
+                    out=y_bf[:].rearrange("p (c i t) -> p c t i", i=4, t=PACK),
+                    in_=y_sb[:].rearrange("p t (c i) -> p c t i", i=4),
+                )
+                y_c = tile("y_c%d_%d" % (g, c), [P, HALF], U32)
+                nc.vector.quantize_mx(out=y_c[:].bitcast(FP8X4), scales=y_s[:, g, cols], in_=y_bf[:])
+                nc.sync.dma_start(
+                    out=out_1[g].rearrange("p m t -> p (m t)").bitcast(I32)[:, cols], in_=y_c[:].bitcast(I32)
+                )
+        for q in range(4):
+            queue = nc.sync if q % 2 == 0 else nc.scalar
+            queue.dma_start(
+                out=out_2[:, 4 * q : 4 * q + 4, :].rearrange("g r n -> r g n").bitcast(I32),
+                in_=y_s[32 * q : 32 * q + 4, :, :].bitcast(I32),
+            )

@@ -22,7 +22,8 @@ PASSES = K // (P * PACK)
 BANK = 512
 HALF = PICK // 2
 GROUPS = N // (P * PACK)
-LIVE = 32 - 4 * PASSES
+CARRIED = 112
+PIECE = 32
 
 
 def tile_list_discard_danger_kernel(
@@ -44,115 +45,115 @@ def tile_list_discard_danger_kernel(
         pos1_sb = sb.tile([P, PICK // 16], U16, name="pos1_sb")
         pos2_sb = sb.tile([P, PICK // 16], U16, name="pos2_sb")
 
-        def streamed(name, shape, dtype):
-            return sb.tile(shape, dtype, name=name, tag="stream", bufs=3, align_bytes=64)
-
         tab_s = tile("tab_s", [P, T], U8)
         w2_s_raw = tile("w2_s_raw", [P, PASSES, H], U8)
-        v_s_packed = tile("v_s_packed", [P, S], U8)
-        v_s = [tile("v_s%d" % a, [P, S], U8) for a in range(PASSES)]
-        nc.vector.memset(w2_s_raw[:].bitcast(I32), 0)
-        for q in range(4):
-            nc.vector.memset(tab_s[32 * q : 32 * q + LIVE, :].bitcast(I32), 0)
-        for a in range(PASSES):
-            nc.vector.memset(v_s[a][:].bitcast(I32), 0)
-
-        nc.sync.dma_start(offs_sb[:], offs)
-        nc.sync.dma_start(pos2_sb[:], pos2)
-        nc.sync.dma_start(pos1_sb[:], pos1)
-        for q in range(4):
-            nc.scalar.dma_start(
-                out=tab_s[32 * q + LIVE : 32 * (q + 1), :].bitcast(I32),
-                in_=tab_scales[:, 4 * q : 4 * q + 4, :].bitcast(I32),
-            )
-
-        tab_w = [streamed("tab_w%d" % a, [P, T], I32) for a in range(PASSES)]
-        w2_raw = tile("w2_raw", [P, PASSES, 2 * H], U8)
+        nc.gpsimd.memset(w2_s_raw[:].bitcast(I32), 0)
+        nc.vector.memset(tab_s[:].bitcast(I32), 0)
 
         def load_tab(a):
-            nc.sync.dma_start(out=tab_w[a][:], in_=tab_words[a].rearrange("p t i -> p (t i)").bitcast(I32))
+            words = tile("tab_w%d" % a, [P, T], I32)
+            nc.sync.dma_start(out=words[:], in_=tab_words[a].rearrange("p t i -> p (t i)").bitcast(I32))
+            return words
 
-        load_tab(0)
-        nc.sync.dma_start(out=w2_raw[:].bitcast(I32), in_=w2_words.rearrange("a p n -> p a n").bitcast(I32))
+        def load_rows(name, rows_ap):
+            raw = tile(name, [P, PACK, H], F32)
+            nc.sync.dma_start(out=raw[:], in_=rows_ap)
+            return raw
+
+        def load_w1(a):
+            return load_rows(
+                "w1_raw%d" % a, w1[a * P * PACK : (a + 1) * P * PACK, :].rearrange("(p i) r -> p i r", i=PACK)
+            )
+
+        def load_w6(g):
+            return load_rows("w6_raw%d" % g, w6.rearrange("(p i) n -> p i n", i=PACK)[:, :, g * H : (g + 1) * H])
+
+        def load_row_values(name, vec):
+            values = tile(name, [P, PACK], F32)
+            nc.sync.dma_start(out=values[:], in_=vec.rearrange("(p t) -> p t", t=PACK))
+            return values
+
+        nc.sync.dma_start(offs_sb[:], offs)
         for q in range(4):
             nc.sync.dma_start(
                 out=w2_s_raw[32 * q : 32 * q + 4, :, :].bitcast(I32),
                 in_=w2_scales[:, 4 * q : 4 * q + 4, :].rearrange("a r n -> r a n").bitcast(I32),
             )
-        load_tab(1)
-        load_tab(2)
-
-        nc.vector.tensor_copy(out=v_s_packed[:], in_=tab_s[:].indirect(offs_sb[:]))
-        for a in range(PASSES):
-            first = LIVE + 4 * a
-            nc.scalar.dma_start(
-                out=v_s[a][0 : P - first, :].bitcast(I32), in_=v_s_packed[first:P, :].bitcast(I32)
+        tab_w = [load_tab(0), load_tab(1)]
+        w1_raw = [load_w1(0)]
+        for q in range(4):
+            nc.sync.dma_start(
+                out=tab_s[32 * q : 32 * q + 4 * PASSES, :].bitcast(I32),
+                in_=tab_scales[:, 4 * q : 4 * q + 4, :].bitcast(I32),
             )
+        tab_w.append(load_tab(2))
+        nc.sync.dma_start(pos1_sb[:], pos1)
+        w1_raw.append(load_w1(1))
+        nc.sync.dma_start(pos2_sb[:], pos2)
+        w1_last = []
+        for half in range(2):
+            raw = tile("w1_last%d" % half, [P, PACK, H // 2], F32)
+            rows = w1[2 * P * PACK :, half * H // 2 : (half + 1) * H // 2]
+            nc.sync.dma_start(out=raw[:], in_=rows.rearrange("(p i) r -> p i r", i=PACK))
+            w1_last.append(raw)
+        sharp_sb = load_row_values("sharp_sb", sharp)
+        share_sb = load_row_values("share_sb", share)
+        w2_raw = tile("w2_raw", [P, PASSES, 2 * H], U8)
+        nc.sync.dma_start(out=w2_raw[:].bitcast(I32), in_=w2_words.rearrange("a p n -> p a n").bitcast(I32))
+        w6_raw = [load_w6(0)]
+
         w2_s = tile("w2_s", [P, PASSES, H], U8)
         nc.vector.tensor_copy(
             out=w2_s[:].rearrange("p a (t m) -> p a t m", t=PACK),
             in_=w2_s_raw[:].rearrange("p a (m t) -> p a t m", t=PACK),
         )
-        w2_c = tile("w2_c", [P, PASSES, 2 * H], U8)
-        nc.scalar.copy(
-            out=w2_c[:].bitcast(U16).rearrange("p a (t m) -> p a t m", t=PACK),
-            in_=w2_raw[:].bitcast(U16).rearrange("p a (m t) -> p a t m", t=PACK),
-        )
-
-        def load_rows(name, rows_ap):
-            raw = streamed(name, [P, PACK, H], F32)
-            nc.sync.dma_start(out=raw[:], in_=rows_ap)
-            return raw
-
-        w1_raw = [
-            load_rows("w1_raw%d" % a, w1[a * P * PACK : (a + 1) * P * PACK, :].rearrange("(p i) r -> p i r", i=PACK))
-            for a in range(PASSES)
-        ]
-        row_values = tile("row_values", [P, 4, 8], F32, "v_s_packed")
-        rows = {}
-        for n, (name, vec) in enumerate((("tilt", tilt), ("sharp", sharp), ("share", share), ("base", base))):
-            rows[name] = row_values[:, n, 0:PACK]
-            nc.sync.dma_start(out=rows[name], in_=vec.rearrange("(p t) -> p t", t=PACK))
-        turn_sb = load_rows("turn_sb", turn.rearrange("(p t) m -> p t m", t=PACK))
-        w6_raw = [
-            load_rows("w6_raw%d" % g, w6.rearrange("(p i) n -> p i n", i=PACK)[:, :, g * H : (g + 1) * H])
-            for g in range(GROUPS)
-        ]
 
         v_w = [[tile("v_w%d_%d" % (a, j), [P, BANK], U32) for j in range(2)] for a in range(PASSES)]
-        g_bank = [[bank("g_ps%d_%d" % (t, j), 2 * t + j) for j in range(2)] for t in range(PACK)]
-        for a in range(PASSES):
+
+        def gather_words(a):
             for j in range(2):
                 nc.vector.tensor_copy(
                     out=v_w[a][j][:],
                     in_=tab_w[a][:].bitcast(U32).indirect(offs_sb[:, j * BANK // 16 : (j + 1) * BANK // 16]),
                 )
 
-        def g_pass(a, t, j):
-            nc.tensor.matmul_mx(
-                out=g_bank[t][j][:],
-                lhsT=w2_c[:, a, 2 * P * t : 2 * P * (t + 1)].bitcast(FP4X4),
-                lhsT_scale=w2_s[:, a, P * t : P * (t + 1)],
-                rhs=v_w[a][j][:].bitcast(FP8X4),
-                rhs_scale=v_s[a][:, j * BANK : (j + 1) * BANK],
-                start=(a == 0),
-                stop=(a == PASSES - 1),
+        gather_words(0)
+        gather_words(1)
+        v_s = tile("v_s", [P, S], U8)
+        nc.vector.tensor_copy(out=v_s[:], in_=tab_s[:].indirect(offs_sb[:]))
+        gather_words(2)
+        carried = tile("carried", [P, PASSES - 1, S], U8)
+        for a in range(1, PASSES):
+            nc.scalar.dma_start(
+                out=carried[0:CARRIED, a - 1, :].bitcast(I32), in_=v_s[4 * a : 4 * a + CARRIED, :].bitcast(I32)
             )
+        base_sb = load_row_values("base_sb", base)
+        tilt_sb = load_row_values("tilt_sb", tilt)
+        turn_sb = load_rows("turn_sb", turn.rearrange("(p t) m -> p t m", t=PACK))
+        w6_raw.append(load_w6(1))
 
-        for a in range(PASSES - 1):
-            for j in range(2):
-                for t in range(PACK):
-                    g_pass(a, t, j)
-        for t in range(PACK):
-            for j in range(2):
-                g_pass(PASSES - 1, t, j)
+        def on_scalar(out, in_):
+            nc.scalar.copy(out=out, in_=in_)
 
-        def round_weight(engine_copy, name, raw):
+        def on_scalar_act(out, in_):
+            nc.scalar.activation(out=out, in_=in_, func=ACT.Copy)
+
+        def on_vector(out, in_):
+            nc.vector.tensor_copy(out=out, in_=in_)
+
+        def on_gpsimd(out, in_):
+            nc.gpsimd.tensor_scalar(out=out, in0=in_, scalar1=1.0, scalar2=0.0, op0=ALU.mult, op1=ALU.add)
+
+        def by_column_group(raw):
+            return raw[:].rearrange("p i (m t) -> p m t i", t=PACK)
+
+        def round_weight(name, shares):
             dealt = tile(name + "_bf", [P, PACK * H], BF16)
-            engine_copy(
-                out=dealt[:].rearrange("p (t m i) -> p m t i", t=PACK, i=PACK),
-                in_=raw[:].rearrange("p i (m t) -> p m t i", t=PACK),
-            )
+            out = dealt[:].rearrange("p (t m i) -> p m t i", t=PACK, i=PACK)
+            first = 0
+            for copy, part in shares:
+                copy(out[:, first : first + part.shape[1]], part)
+                first = first + part.shape[1]
             return dealt
 
         def quantise(name, values, width):
@@ -161,8 +162,8 @@ def tile_list_discard_danger_kernel(
             nc.vector.quantize_mx(out=codes[:].bitcast(FP8X4), scales=scales[:], in_=values[:])
             return codes, scales
 
-        def empty(name, banks, tag=None):
-            whole = tile(name, [P, S], F32, tag)
+        def empty(name, banks):
+            whole = tile(name, [P, S], F32)
             top = tile(name + "_top", [P, 2], F32)
             for j in range(2):
                 nc.vector.tensor_scalar(
@@ -171,49 +172,37 @@ def tile_list_discard_danger_kernel(
                 )
             return whole, top
 
-        def scalar_round(out, in_):
-            nc.scalar.activation(out=out, in_=in_, func=ACT.Copy)
-
-        w1_bf = [round_weight(scalar_round, "w1_%d" % a, w1_raw[a]) for a in range(2)]
-
-        exp_bias = tile("exp_bias", [P, PACK], F32)
-        c_sb = []
-        for t in range(PACK):
-            g_sb, top = empty("g%d" % t, g_bank[t])
-            nc.vector.tensor_scalar(
-                out=exp_bias[:, t : t + 1], in0=top[:, 0:1], scalar1=top[:, 1:2], scalar2=-1.0,
-                op0=ALU.max, op1=ALU.mult,
-            )
-            c_t = tile("c%d" % t, [P, PICK], F32)
-            nc.scalar.activation(
-                out=c_t[:], in_=g_sb[:].indirect(pos2_sb[:]), func=ACT.Exp, bias=exp_bias[:, t : t + 1]
-            )
-            c_sb.append(c_t)
-
-        w1_q = [quantise("w1_%d" % a, w1_bf[a], H) for a in range(2)]
-        w1_bf.append(round_weight(nc.vector.tensor_copy, "w1_2", w1_raw[2]))
-        gain = tile("gain", [P, PACK], F32)
-        nc.vector.scalar_tensor_tensor(
-            out=gain[:], in0=rows["sharp"], scalar=-1.0, in1=rows["share"], op0=ALU.mult, op1=ALU.mult
+        w1_shares = (
+            [(on_scalar, by_column_group(w1_raw[0]))],
+            [(on_vector, by_column_group(w1_raw[1])[:, 0 : P // 2]), (on_scalar, by_column_group(w1_raw[1])[:, P // 2 : P])],
+            [(on_scalar, by_column_group(w1_last[0])), (on_vector, by_column_group(w1_last[1]))],
         )
-        w1_q.append(quantise("w1_2", w1_bf[2], H))
+        w1_q = [quantise("w1_%d" % a, round_weight("w1_%d" % a, w1_shares[a]), H) for a in range(PASSES)]
 
         h_bank = [[bank("h_ps%d_%d" % (t, j), 2 * t + j) for j in range(2)] for t in range(PACK)]
-        for a in range(PASSES):
-            for t in range(PACK):
-                for j in range(2):
+        for t in range(PACK):
+            for j in range(2):
+                for a in range(PASSES):
                     nc.tensor.matmul_mx(
                         out=h_bank[t][j][:],
                         lhsT=w1_q[a][0][:, P * t : P * (t + 1)].bitcast(FP8X4),
                         lhsT_scale=w1_q[a][1][:, P * t : P * (t + 1)],
                         rhs=v_w[a][j][:].bitcast(FP8X4),
-                        rhs_scale=v_s[a][:, j * BANK : (j + 1) * BANK],
+                        rhs_scale=v_s[4 * a : P, j * BANK : (j + 1) * BANK],
                         start=(a == 0),
                         stop=(a == PASSES - 1),
                     )
 
+        w2_c = tile("w2_c", [P, PASSES, 2 * H], U8)
+        nc.scalar.copy(
+            out=w2_c[:].bitcast(U16).rearrange("p a (t m) -> p a t m", t=PACK),
+            in_=w2_raw[:].bitcast(U16).rearrange("p a (m t) -> p a t m", t=PACK),
+        )
+        gain = tile("gain", [P, PACK], F32)
+        nc.vector.scalar_tensor_tensor(
+            out=gain[:], in0=sharp_sb[:], scalar=-1.0, in1=share_sb[:], op0=ALU.mult, op1=ALU.mult
+        )
 
-        w6_bf = [round_weight(scalar_round, "w6_0", w6_raw[0])]
         sig_bias = tile("sig_bias", [P, PACK], F32)
         a_sb = []
         for t in range(PACK):
@@ -222,72 +211,131 @@ def tile_list_discard_danger_kernel(
                 out=sig_bias[:, t : t + 1], in0=top[:, 0:1], scalar1=top[:, 1:2], scalar2=gain[:, t : t + 1],
                 op0=ALU.max, op1=ALU.mult,
             )
-            halves = []
-            for c in range(2):
-                a_t = tile("a%d_%d" % (t, c), [P, HALF], F32)
-                nc.scalar.activation(
-                    out=a_t[:], in_=h_sb[:].indirect(pos1_sb[:, c * HALF // 16 : (c + 1) * HALF // 16]),
-                    func=ACT.Sigmoid, bias=sig_bias[:, t : t + 1], scale=rows["sharp"][:, t : t + 1],
-                )
-                halves.append(a_t)
-            a_sb.append(halves)
-
-        w6_bf.append(round_weight(nc.vector.tensor_copy, "w6_1", w6_raw[1]))
-        weighted = []
-        for t in range(PACK):
-            w_t = tile("weighted%d" % t, [P, PICK], F32)
-            nc.vector.scalar_tensor_tensor(
-                out=w_t[:], in0=c_sb[t][:], scalar=rows["tilt"][:, t : t + 1], in1=turn_sb[:, t, :],
-                op0=ALU.subtract, op1=ALU.mult,
+            a_t = tile("a%d" % t, [P, PICK], F32)
+            nc.scalar.activation(
+                out=a_t[:], in_=h_sb[:].indirect(pos1_sb[:]), func=ACT.Sigmoid,
+                bias=sig_bias[:, t : t + 1], scale=sharp_sb[:, t : t + 1],
             )
-            weighted.append(w_t)
-        w6_q = [quantise("w6_%d" % g, w6_bf[g], H) for g in range(GROUPS)]
+            a_sb.append(a_t)
 
+        g_bank = [[bank("g_ps%d_%d" % (t, j), 2 * t + j) for j in range(2)] for t in range(PACK)]
+        for t in range(PACK):
+            for j in range(2):
+                cols = slice(j * BANK, (j + 1) * BANK)
+                for a in range(PASSES):
+                    nc.tensor.matmul_mx(
+                        out=g_bank[t][j][:],
+                        lhsT=w2_c[:, a, 2 * P * t : 2 * P * (t + 1)].bitcast(FP4X4),
+                        lhsT_scale=w2_s[:, a, P * t : P * (t + 1)],
+                        rhs=v_w[a][j][:].bitcast(FP8X4),
+                        rhs_scale=v_s[:, cols] if a == 0 else carried[:, a - 1, cols],
+                        start=(a == 0),
+                        stop=(a == PASSES - 1),
+                    )
+
+        def round_w6(g):
+            whole = by_column_group(w6_raw[g])
+            return round_weight("w6_%d" % g, [(on_gpsimd, whole[:, m : m + PIECE]) for m in range(0, P, PIECE)])
+
+        def weigh(c, on_g):
+            cols = slice(c * HALF, (c + 1) * HALF)
+            weighted = tile("weighted%d" % c, [P, PACK, HALF], F32)
+            for t in range(PACK):
+                if on_g:
+                    off = tile("off%d_%d" % (c, t), [P, HALF], F32, "off%d" % (t % 2))
+                    nc.gpsimd.tensor_scalar(
+                        out=off[:], in0=a_sb[t][:, cols], scalar1=less_base[:, t : t + 1], scalar2=1.0,
+                        op0=ALU.add, op1=ALU.mult,
+                    )
+                    nc.gpsimd.tensor_tensor(out=weighted[:, t, :], in0=off[:], in1=turn_sb[:, t, cols], op=ALU.mult)
+                else:
+                    nc.vector.scalar_tensor_tensor(
+                        out=weighted[:, t, :], in0=a_sb[t][:, cols], scalar=base_sb[:, t : t + 1],
+                        in1=turn_sb[:, t, cols], op0=ALU.subtract, op1=ALU.mult,
+                    )
+            return weighted
+
+        less_base = base_sb
+
+        exp_bias = tile("exp_bias", [P, PACK], F32)
+        g_sb = []
+
+        def look(t, c):
+            c_t = tile("c%d_%d" % (t, c), [P, HALF], F32)
+            nc.scalar.activation(
+                out=c_t[:], in_=g_sb[t][:].indirect(pos2_sb[:, c * HALF // 16 : (c + 1) * HALF // 16]),
+                func=ACT.Exp, bias=exp_bias[:, t : t + 1],
+            )
+            return c_t
+
+        c_sb = []
+        for t in range(PACK):
+            whole, top = empty("g%d" % t, g_bank[t])
+            g_sb.append(whole)
+            nc.vector.tensor_scalar(
+                out=exp_bias[:, t : t + 1], in0=top[:, 0:1], scalar1=top[:, 1:2], scalar2=-1.0,
+                op0=ALU.max, op1=ALU.mult,
+            )
+            c_sb.append([look(t, 0)])
+        for t in range(PACK):
+            c_sb[t].append(look(t, 1))
+
+        w6_bf = [round_w6(0)]
+        weighted_all = []
+        w6_bf.append(round_w6(1))
+        w6_q = [quantise("w6_0", w6_bf[0], H)]
         z_q = []
         for c in range(2):
+            cols = slice(c * HALF, (c + 1) * HALF)
+            weighted = weighted_all[c] if c < len(weighted_all) else weigh(c, False)
             z_rows = tile("z_rows%d" % c, [P, PACK, HALF], BF16)
             for t in range(PACK):
                 nc.vector.scalar_tensor_tensor(
-                    out=z_rows[:, t, :], in0=a_sb[t][c][:], scalar=rows["base"][:, t : t + 1],
-                    in1=weighted[t][:, c * HALF : (c + 1) * HALF], op0=ALU.subtract, op1=ALU.mult,
+                    out=z_rows[:, t, :], in0=c_sb[t][c][:], scalar=tilt_sb[:, t : t + 1],
+                    in1=weighted[:, t, :], op0=ALU.subtract, op1=ALU.mult,
                 )
             z_bf = tile("z_bf%d" % c, [P, PACK * HALF], BF16)
-            nc.vector.tensor_copy(
-                out=z_bf[:].rearrange("p (c i t) -> p c t i", i=4, t=PACK),
-                in_=z_rows[:].rearrange("p t (c i) -> p c t i", i=4),
+            (on_vector if c == 0 else on_scalar)(
+                z_bf[:].rearrange("p (c i t) -> p c t i", i=4, t=PACK),
+                z_rows[:].rearrange("p t (c i) -> p c t i", i=4),
             )
             z_q.append(quantise("z%d" % c, z_bf, HALF))
+            if c == 0:
+                w6_q.append(quantise("w6_1", w6_bf[1], H))
 
+        spare = ["tab_w0", "tab_w1", "tab_w2", "w1_raw0"]
         y_s = tile("y_s", [P, GROUPS, PICK], U8)
         y_rows = out_0.rearrange("(g p t) m -> g p t m", p=P, t=PACK)
         for c in range(2):
             cols = slice(c * HALF, (c + 1) * HALF)
             for g in range(GROUPS):
-                y_sb = tile("y%d_%d" % (g, c), [P, PACK, HALF], F32)
+                y_sb = tile("y%d_%d" % (g, c), [P, PACK, HALF], F32, spare[2 * c + g])
+                y_c = tile("y_c%d_%d" % (g, c), [P, HALF], U32)
                 for u in range(2):
+                    part = slice(u * P, (u + 1) * P)
                     y_ps = bank("y_ps%d_%d_%d" % (c, g, u), 4 * c + 2 * g + u)
-                    for e in range(2):
-                        t = 2 * u + e
+                    for t in range(PACK):
                         nc.tensor.matmul_mx(
-                            out=y_ps[:, e * HALF : (e + 1) * HALF],
+                            out=y_ps[:, t * P : (t + 1) * P],
                             lhsT=w6_q[g][0][:, P * t : P * (t + 1)].bitcast(FP8X4),
                             lhsT_scale=w6_q[g][1][:, P * t : P * (t + 1)],
-                            rhs=z_q[c][0][:].bitcast(FP8X4),
-                            rhs_scale=z_q[c][1][:],
+                            rhs=z_q[c][0][:, part].bitcast(FP8X4),
+                            rhs_scale=z_q[c][1][:, part],
                             start=True,
                             stop=True,
                         )
-                    nc.scalar.copy(
-                        out=y_sb[:, 2 * u : 2 * u + 2, :], in_=y_ps[:].rearrange("p (e m) -> p e m", e=2)
+                    nc.scalar.copy(out=y_sb[:, :, part], in_=y_ps[:].rearrange("p (t m) -> p t m", t=PACK))
+                    y_bf = tile("y_bf%d_%d_%d" % (g, c, u), [P, PACK * P], BF16)
+                    nc.vector.tensor_copy(
+                        out=y_bf[:].rearrange("p (c i t) -> p c t i", i=4, t=PACK),
+                        in_=y_sb[:, :, part].rearrange("p t (c i) -> p c t i", i=4),
+                    )
+                    nc.vector.quantize_mx(
+                        out=y_c[:, part].bitcast(FP8X4),
+                        scales=y_s[:, g, c * HALF + u * P : c * HALF + (u + 1) * P],
+                        in_=y_bf[:],
                     )
                 nc.sync.dma_start(out=y_rows[g][:, :, cols], in_=y_sb[:])
-                y_bf = tile("y_bf%d_%d" % (g, c), [P, PACK * HALF], BF16)
-                nc.vector.tensor_copy(
-                    out=y_bf[:].rearrange("p (c i t) -> p c t i", i=4, t=PACK),
-                    in_=y_sb[:].rearrange("p t (c i) -> p c t i", i=4),
-                )
-                y_c = tile("y_c%d_%d" % (g, c), [P, HALF], U32)
-                nc.vector.quantize_mx(out=y_c[:].bitcast(FP8X4), scales=y_s[:, g, cols], in_=y_bf[:])
                 nc.sync.dma_start(
                     out=out_1[g].rearrange("p m t -> p (m t)").bitcast(I32)[:, cols], in_=y_c[:].bitcast(I32)
                 )

from contextlib import ExitStack

import concourse.mybir as mybir

K, H, N, T, S, PICK = 1536, 512, 1024, 2048, 1024, 512
FLOPS = 2 * (2 * K * H * S + H * N * PICK)

F32 = mybir.dt.float32
BF16 = mybir.dt.bfloat16
I32 = mybir.dt.int32
U32 = mybir.dt.uint32
U16 = mybir.dt.uint16
U8 = mybir.dt.uint8
FP8X4 = mybir.dt.float8_e4m3fn_x4
FP4X4 = mybir.dt.float4_e2m1fn_x4
ALU = mybir.AluOpType
ACT = mybir.ActivationFunctionType

P = 128
PACK = 4
PASSES = K // (P * PACK)
BANK = 512
HALF = PICK // 2
GROUPS = N // (P * PACK)
CARRIED = 112
PIECE = 32


def tile_list_discard_danger_kernel(
    tc, tab_words, tab_scales, offs, pos1, pos2, w1, w2_words, w2_scales, w6,
    sharp, share, base, tilt, turn, out_0, out_1, out_2,
):
    nc = tc.nc
    with ExitStack() as ctx:
        sb = ctx.enter_context(tc.tile_pool(name="sb", bufs=1))
        ps = ctx.enter_context(tc.psum_pool(name="ps", bufs=1))

        def tile(name, shape, dtype, tag=None):
            return sb.tile(shape, dtype, name=name, tag=tag or name, align_bytes=64)

        def bank(name, b):
            return ps.tile([P, BANK], F32, name=name, tag="bank%d" % b)

        offs_sb = sb.tile([P, S // 16], U16, name="offs_sb")
        pos1_sb = sb.tile([P, PICK // 16], U16, name="pos1_sb")
        pos2_sb = sb.tile([P, PICK // 16], U16, name="pos2_sb")

        tab_s = tile("tab_s", [P, T], U8)
        w2_s_raw = tile("w2_s_raw", [P, PASSES, H], U8)
        nc.gpsimd.memset(w2_s_raw[:].bitcast(I32), 0)
        nc.vector.memset(tab_s[:].bitcast(I32), 0)

        def load_tab(a):
            words = tile("tab_w%d" % a, [P, T], I32)
            nc.sync.dma_start(out=words[:], in_=tab_words[a].rearrange("p t i -> p (t i)").bitcast(I32))
            return words

        def load_rows(name, rows_ap):
            raw = tile(name, [P, PACK, H], F32)
            nc.sync.dma_start(out=raw[:], in_=rows_ap)
            return raw

        def load_w1(a):
            return load_rows(
                "w1_raw%d" % a, w1[a * P * PACK : (a + 1) * P * PACK, :].rearrange("(p i) r -> p i r", i=PACK)
            )

        def load_w6(g):
            return load_rows("w6_raw%d" % g, w6.rearrange("(p i) n -> p i n", i=PACK)[:, :, g * H : (g + 1) * H])

        def load_row_values(name, vec):
            values = tile(name, [P, PACK], F32)
            nc.sync.dma_start(out=values[:], in_=vec.rearrange("(p t) -> p t", t=PACK))
            return values

        nc.sync.dma_start(offs_sb[:], offs)
        for q in range(4):
            nc.sync.dma_start(
                out=w2_s_raw[32 * q : 32 * q + 4, :, :].bitcast(I32),
                in_=w2_scales[:, 4 * q : 4 * q + 4, :].rearrange("a r n -> r a n").bitcast(I32),
            )
        tab_w = [load_tab(0), load_tab(1)]
        w1_raw = [load_w1(0)]
        for q in range(4):
            nc.sync.dma_start(
                out=tab_s[32 * q : 32 * q + 4 * PASSES, :].bitcast(I32),
                in_=tab_scales[:, 4 * q : 4 * q + 4, :].bitcast(I32),
            )
        tab_w.append(load_tab(2))
        nc.sync.dma_start(pos1_sb[:], pos1)
        w1_raw.append(load_w1(1))
        nc.sync.dma_start(pos2_sb[:], pos2)
        w1_last = []
        for half in range(2):
            raw = tile("w1_last%d" % half, [P, PACK, H // 2], F32)
            rows = w1[2 * P * PACK :, half * H // 2 : (half + 1) * H // 2]
            nc.sync.dma_start(out=raw[:], in_=rows.rearrange("(p i) r -> p i r", i=PACK))
            w1_last.append(raw)
        sharp_sb = load_row_values("sharp_sb", sharp)
        share_sb = load_row_values("share_sb", share)
        w2_raw = tile("w2_raw", [P, PASSES, 2 * H], U8)
        nc.sync.dma_start(out=w2_raw[:].bitcast(I32), in_=w2_words.rearrange("a p n -> p a n").bitcast(I32))
        w6_raw = [load_w6(0)]

        w2_s = tile("w2_s", [P, PASSES, H], U8)
        nc.vector.tensor_copy(
            out=w2_s[:].rearrange("p a (t m) -> p a t m", t=PACK),
            in_=w2_s_raw[:].rearrange("p a (m t) -> p a t m", t=PACK),
        )

        v_w = [[tile("v_w%d_%d" % (a, j), [P, BANK], U32) for j in range(2)] for a in range(PASSES)]

        def gather_words(a):
            for j in range(2):
                nc.vector.tensor_copy(
                    out=v_w[a][j][:],
                    in_=tab_w[a][:].bitcast(U32).indirect(offs_sb[:, j * BANK // 16 : (j + 1) * BANK // 16]),
                )

        gather_words(0)
        gather_words(1)
        v_s = tile("v_s", [P, S], U8)
        nc.vector.tensor_copy(out=v_s[:], in_=tab_s[:].indirect(offs_sb[:]))
        gather_words(2)
        carried = tile("carried", [P, PASSES - 1, S], U8)
        for a in range(1, PASSES):
            nc.scalar.dma_start(
                out=carried[0:CARRIED, a - 1, :].bitcast(I32), in_=v_s[4 * a : 4 * a + CARRIED, :].bitcast(I32)
            )
        base_sb = load_row_values("base_sb", base)
        tilt_sb = load_row_values("tilt_sb", tilt)
        turn_sb = load_rows("turn_sb", turn.rearrange("(p t) m -> p t m", t=PACK))
        w6_raw.append(load_w6(1))

        def on_scalar(out, in_):
            nc.scalar.copy(out=out, in_=in_)

        def on_scalar_act(out, in_):
            nc.scalar.activation(out=out, in_=in_, func=ACT.Copy)

        def on_vector(out, in_):
            nc.vector.tensor_copy(out=out, in_=in_)

        def on_gpsimd(out, in_):
            nc.gpsimd.tensor_scalar(out=out, in0=in_, scalar1=1.0, scalar2=0.0, op0=ALU.mult, op1=ALU.add)

        def by_column_group(raw):
            return raw[:].rearrange("p i (m t) -> p m t i", t=PACK)

        def round_weight(name, shares):
            dealt = tile(name + "_bf", [P, PACK * H], BF16)
            out = dealt[:].rearrange("p (t m i) -> p m t i", t=PACK, i=PACK)
            first = 0
            for copy, part in shares:
                copy(out[:, first : first + part.shape[1]], part)
                first = first + part.shape[1]
            return dealt

        def quantise(name, values, width):
            codes = tile(name + "_c", [P, width], U32)
            scales = tile(name + "_s", [P, width], U8)
            nc.vector.quantize_mx(out=codes[:].bitcast(FP8X4), scales=scales[:], in_=values[:])
            return codes, scales

        def empty(name, banks):
            whole = tile(name, [P, S], F32)
            top = tile(name + "_top", [P, 2], F32)
            for j in range(2):
                nc.vector.tensor_scalar(
                    out=whole[:, j * BANK : (j + 1) * BANK], in0=banks[j][:], scalar1=1.0, scalar2=None,
                    op0=ALU.mult, op1=ALU.max, accum_out=top[:, j : j + 1],
                )
            return whole, top

        w1_shares = (
            [(on_scalar, by_column_group(w1_raw[0]))],
            [(on_vector, by_column_group(w1_raw[1])[:, 0 : P // 2]), (on_scalar, by_column_group(w1_raw[1])[:, P // 2 : P])],
            [(on_scalar, by_column_group(w1_last[0])), (on_vector, by_column_group(w1_last[1]))],
        )
        w1_q = [quantise("w1_%d" % a, round_weight("w1_%d" % a, w1_shares[a]), H) for a in range(PASSES)]

        h_bank = [[bank("h_ps%d_%d" % (t, j), 2 * t + j) for j in range(2)] for t in range(PACK)]
        for t in range(PACK):
            for j in range(2):
                for a in range(PASSES):
                    nc.tensor.matmul_mx(
                        out=h_bank[t][j][:],
                        lhsT=w1_q[a][0][:, P * t : P * (t + 1)].bitcast(FP8X4),
                        lhsT_scale=w1_q[a][1][:, P * t : P * (t + 1)],
                        rhs=v_w[a][j][:].bitcast(FP8X4),
                        rhs_scale=v_s[4 * a : P, j * BANK : (j + 1) * BANK],
                        start=(a == 0),
                        stop=(a == PASSES - 1),
                    )

        w2_c = tile("w2_c", [P, PASSES, 2 * H], U8)
        nc.scalar.copy(
            out=w2_c[:].bitcast(U16).rearrange("p a (t m) -> p a t m", t=PACK),
            in_=w2_raw[:].bitcast(U16).rearrange("p a (m t) -> p a t m", t=PACK),
        )
        gain = tile("gain", [P, PACK], F32)
        nc.vector.scalar_tensor_tensor(
            out=gain[:], in0=sharp_sb[:], scalar=-1.0, in1=share_sb[:], op0=ALU.mult, op1=ALU.mult
        )

        sig_bias = tile("sig_bias", [P, PACK], F32)
        a_sb = []
        for t in range(PACK):
            h_sb, top = empty("h%d" % t, h_bank[t])
            nc.vector.tensor_scalar(
                out=sig_bias[:, t : t + 1], in0=top[:, 0:1], scalar1=top[:, 1:2], scalar2=gain[:, t : t + 1],
                op0=ALU.max, op1=ALU.mult,
            )
            a_t = tile("a%d" % t, [P, PICK], F32)
            nc.scalar.activation(
                out=a_t[:], in_=h_sb[:].indirect(pos1_sb[:]), func=ACT.Sigmoid,
                bias=sig_bias[:, t : t + 1], scale=sharp_sb[:, t : t + 1],
            )
            a_sb.append(a_t)

        g_bank = [[bank("g_ps%d_%d" % (t, j), 2 * t + j) for j in range(2)] for t in range(PACK)]
        for t in range(PACK):
            for j in range(2):
                cols = slice(j * BANK, (j + 1) * BANK)
                for a in range(PASSES):
                    nc.tensor.matmul_mx(
                        out=g_bank[t][j][:],
                        lhsT=w2_c[:, a, 2 * P * t : 2 * P * (t + 1)].bitcast(FP4X4),
                        lhsT_scale=w2_s[:, a, P * t : P * (t + 1)],
                        rhs=v_w[a][j][:].bitcast(FP8X4),
                        rhs_scale=v_s[:, cols] if a == 0 else carried[:, a - 1, cols],
                        start=(a == 0),
                        stop=(a == PASSES - 1),
                    )

        def round_w6(g):
            whole = by_column_group(w6_raw[g])
            return round_weight("w6_%d" % g, [(on_gpsimd, whole[:, m : m + PIECE]) for m in range(0, P, PIECE)])

        def weigh(c, on_g):
            cols = slice(c * HALF, (c + 1) * HALF)
            weighted = tile("weighted%d" % c, [P, PACK, HALF], F32)
            for t in range(PACK):
                if on_g:
                    off = tile("off%d_%d" % (c, t), [P, HALF], F32, "off%d" % (t % 2))
                    nc.gpsimd.tensor_scalar(
                        out=off[:], in0=a_sb[t][:, cols], scalar1=less_base[:, t : t + 1], scalar2=1.0,
                        op0=ALU.add, op1=ALU.mult,
                    )
                    nc.gpsimd.tensor_tensor(out=weighted[:, t, :], in0=off[:], in1=turn_sb[:, t, cols], op=ALU.mult)
                else:
                    nc.vector.scalar_tensor_tensor(
                        out=weighted[:, t, :], in0=a_sb[t][:, cols], scalar=base_sb[:, t : t + 1],
                        in1=turn_sb[:, t, cols], op0=ALU.subtract, op1=ALU.mult,
                    )
            return weighted

        less_base = base_sb

        exp_bias = tile("exp_bias", [P, PACK], F32)
        g_sb = []

        def look(t, c):
            c_t = tile("c%d_%d" % (t, c), [P, HALF], F32)
            nc.scalar.activation(
                out=c_t[:], in_=g_sb[t][:].indirect(pos2_sb[:, c * HALF // 16 : (c + 1) * HALF // 16]),
                func=ACT.Exp, bias=exp_bias[:, t : t + 1],
            )
            return c_t

        c_sb = []
        for t in range(PACK):
            whole, top = empty("g%d" % t, g_bank[t])
            g_sb.append(whole)
            nc.vector.tensor_scalar(
                out=exp_bias[:, t : t + 1], in0=top[:, 0:1], scalar1=top[:, 1:2], scalar2=-1.0,
                op0=ALU.max, op1=ALU.mult,
            )
            c_sb.append([look(t, 0)])
        for t in range(PACK):
            c_sb[t].append(look(t, 1))

        w6_bf = [round_w6(0)]
        weighted_all = []
        w6_bf.append(round_w6(1))
        w6_q = [quantise("w6_0", w6_bf[0], H)]
        z_q = []
        for c in range(2):
            cols = slice(c * HALF, (c + 1) * HALF)
            weighted = weighted_all[c] if c < len(weighted_all) else weigh(c, False)
            z_rows = tile("z_rows%d" % c, [P, PACK, HALF], BF16)
            for t in range(PACK):
                nc.vector.scalar_tensor_tensor(
                    out=z_rows[:, t, :], in0=c_sb[t][c][:], scalar=tilt_sb[:, t : t + 1],
                    in1=weighted[:, t, :], op0=ALU.subtract, op1=ALU.mult,
                )
            z_bf = tile("z_bf%d" % c, [P, PACK * HALF], BF16)
            (on_vector if c == 0 else on_scalar)(
                z_bf[:].rearrange("p (c i t) -> p c t i", i=4, t=PACK),
                z_rows[:].rearrange("p t (c i) -> p c t i", i=4),
            )
            z_q.append(quantise("z%d" % c, z_bf, HALF))
            if c == 0:
                w6_q.append(quantise("w6_1", w6_bf[1], H))

        spare = ["tab_w0", "tab_w1", "tab_w2", "w1_raw0"]
        y_s = tile("y_s", [P, GROUPS, PICK], U8)
        y_rows = out_0.rearrange("(g p t) m -> g p t m", p=P, t=PACK)
        for c in range(2):
            cols = slice(c * HALF, (c + 1) * HALF)
            for g in range(GROUPS):
                y_sb = tile("y%d_%d" % (g, c), [P, PACK, HALF], F32, spare[2 * c + g])
                y_c = tile("y_c%d_%d" % (g, c), [P, HALF], U32)
                for u in range(2):
                    part = slice(u * P, (u + 1) * P)
                    y_ps = bank("y_ps%d_%d_%d" % (c, g, u), 4 * c + 2 * g + u)
                    for t in range(PACK):
                        nc.tensor.matmul_mx(
                            out=y_ps[:, t * P : (t + 1) * P],
                            lhsT=w6_q[g][0][:, P * t : P * (t + 1)].bitcast(FP8X4),
                            lhsT_scale=w6_q[g][1][:, P * t : P * (t + 1)],
                            rhs=z_q[c][0][:, part].bitcast(FP8X4),
                            rhs_scale=z_q[c][1][:, part],
                            start=True,
                            stop=True,
                        )
                    nc.scalar.copy(out=y_sb[:, :, part], in_=y_ps[:].rearrange("p (t m) -> p t m", t=PACK))
                    y_bf = tile("y_bf%d_%d_%d" % (g, c, u), [P, PACK * P], BF16)
                    nc.vector.tensor_copy(
                        out=y_bf[:].rearrange("p (c i t) -> p c t i", i=4, t=PACK),
                        in_=y_sb[:, :, part].rearrange("p t (c i) -> p c t i", i=4),
                    )
                    nc.vector.quantize_mx(
                        out=y_c[:, part].bitcast(FP8X4),
                        scales=y_s[:, g, c * HALF + u * P : c * HALF + (u + 1) * P],
                        in_=y_bf[:],
                    )
                nc.sync.dma_start(out=y_rows[g][:, :, cols], in_=y_sb[:])
                nc.sync.dma_start(
                    out=out_1[g].rearrange("p m t -> p (m t)").bitcast(I32)[:, cols], in_=y_c[:].bitcast(I32)
                )
        for q in range(4):
            queue = nc.sync if q % 2 == 0 else nc.scalar
            queue.dma_start(
                out=out_2[:, 4 * q : 4 * q + 4, :].rearrange("g r n -> r g n").bitcast(I32),
                in_=y_s[32 * q : 32 * q + 4, :, :].bitcast(I32),
            )
